import numpy as np, ml_dtypes
CORES = [144,200,272,328,400,456]
N = 6
T, G, CAP = 4096, 4096, 1024
def entries(a): return a.T.reshape(-1)
def pack(v, P): return np.ascontiguousarray(np.asarray(v, np.int32).reshape(-1, P).T)
def lists(rng, how):
    S = rng.integers(0, T, (N, 2 * CAP)); P = np.stack([rng.permutation(G)[:2 * CAP] for r in range(N)])
    if how == "alike": S[:] = rng.integers(0, T, (N, 1))
    if how == "edge":
        S = np.where(rng.random((N, 2 * CAP)) < 0.5, 0, T - 1); S[:, [0, CAP]] = 0; S[:, [1, CAP + 1]] = T - 1
        P[:, 1:-1] = np.stack([1 + rng.permutation(G - 2)[:2 * CAP - 2] for r in range(N)]); P[0::2, 0], P[0::2, -1] = 0, G - 1; P[1::2, 0], P[1::2, -1] = G - 1, 0
    if how == "mixed": P = np.stack([rng.permutation(2 * CAP) for r in range(N)]); P[1::2] += G - 2 * CAP
    if how == "sorted":
        S2, P2 = [-np.sort(-A.reshape(N, 2, CAP), axis=2).reshape(N, 2 * CAP) for A in (S, P)]; S, P = -np.sort(-S, axis=1), -np.sort(-P, axis=1)
        S[1::3], P[1::3] = S[1::3, ::-1].copy(), P[1::3, ::-1].copy(); S[2::3], P[2::3] = S2[2::3], P2[2::3]
    return {"snd": np.stack([pack(s, 16) for s in S]), "plc": np.stack([pack(q, 16) for q in P])}
def setup_inputs(rng):
    return dict({"x": rng.standard_normal((N, 128, T), dtype=np.float32).astype(ml_dtypes.bfloat16), "gh": rng.standard_normal((N, 128, G), dtype=np.float32).astype(ml_dtypes.bfloat16)}, **lists(rng, "uniform"))
def setup_inputs_alike(rng):
    d = setup_inputs(rng); d.update(lists(rng, "alike"))
    for k in ("x", "gh"): d[k] = (d[k].astype(np.float32) * 1048576.0).astype(d[k].dtype)
    return d
def setup_inputs_edge(rng):
    d = setup_inputs(rng); d.update(lists(rng, "edge"))
    for k in ("x", "gh"): d[k] = (d[k].astype(np.float32) * (1 / 1024.0)).astype(d[k].dtype)
    return d
def setup_inputs_mixed(rng):
    d = setup_inputs(rng); d.update(lists(rng, "mixed"))
    return d
def setup_inputs_sorted(rng):
    d = setup_inputs(rng); d.update(lists(rng, "sorted"))
    return d
def setup_inputs_zeros(rng):
    d = setup_inputs(rng); d.update(lists(rng, "zeros"))
    for r in range(N): d["x"][r][:, entries(d["snd"][r])[::2]] = 0
    return d
def check_inputs(x):
    bad = []
    if x["snd"].min() < 0 or x["snd"].max() >= T: bad.append("snd out of range")
    if x["plc"].min() < 0 or x["plc"].max() >= G: bad.append("plc out of range")
    if any(len(np.unique(a)) != a.size for a in x["plc"]): bad.append("a place is named twice")
    return bad
def reference(x, gh, snd, plc):
    y = gh.copy()
    for r in range(N):
        S = entries(snd[r]); lo, hi = (r - 1) % N, (r + 1) % N
        y[lo][:, entries(plc[lo])[CAP:]] = x[r][:, S[:CAP]]
        y[hi][:, entries(plc[hi])[:CAP]] = x[r][:, S[CAP:]]
    return {"y": y}

@@ -1,0 +1,371 @@
+from concourse.bass import DstId, RemoteDMATransfer
+from concourse.mybir import AluOpType, ActivationFunctionType
+
+COLS = 4096
+CAP = 1024
+PIECE = 512
+PC = PIECE // 16
+OWNC = 192
+TABC = 64
+
+SCRATCH = {
+    "sndi": ("sbuf", [16, 128], "int32"),
+    "sndf": ("sbuf", [16, 128], "float32"),
+    "repi": ("sbuf", [16, 128], "int32"),
+    "repa": ("sbuf", [16, 128], "int32"),
+    "rep": ("sbuf", [16, 128], "float32"),
+    "soff": ("sbuf", [128, 128], "uint16"),
+    "xs": ("sbuf", [128, 4096], "bfloat16"),
+    "stage": ("sbuf", [128, 2048], "bfloat16"),
+    "gat": ("sbuf", [128, 6144], "bfloat16"),
+    "ys": ("sbuf", [128, 4096], "bfloat16"),
+    "wm": ("sbuf", [128, 192], "uint16"),
+    "wh": ("sbuf", [128, 64], "uint16"),
+    "plci": ("sbuf", [128, 16], "int32"),
+    "poff": ("sbuf", [128, 16], "uint16"),
+    "win": ("sbuf", [128, 4096], "bfloat16"),
+    "hi": ("sbuf", [128, 256], "float32"),
+    "lo": ("sbuf", [128, 256], "float32"),
+    "him": ("sbuf", [128, 256], "float32"),
+    "lom": ("sbuf", [128, 256], "float32"),
+    "val": ("sbuf", [128, 256], "bfloat16"),
+    "pidx": ("sbuf", [128, 8], "int32"),
+    "pmod": ("sbuf", [128, 8], "int32"),
+    "pmf": ("sbuf", [128, 8], "float32"),
+    "is0": ("sbuf", [128, 8], "float32"),
+    "is1": ("sbuf", [128, 8], "float32"),
+    "wf": ("sbuf", [128, 192], "float32"),
+    "wl": ("sbuf", [128, 64], "uint16"),
+    "comb": ("sbuf", [128, 144], "bfloat16"),
+    "plcdef": ("sbuf", [128, 192], "float32"),
+    "combi": ("sbuf", [128, 144], "int32"),
+    "comba": ("sbuf", [128, 144], "int32"),
+    "combs": ("sbuf", [128, 144], "bfloat16"),
+    "defi": ("sbuf", [128, 64], "float32"),
+    "defs": ("sbuf", [128, 64], "float32"),
+    "hop": ("sbuf", [128, 512], "bfloat16"),
+    "psa": ("psum", [128, 512], "float32"),
+    "psw": ("psum", [128, 512], "float32"),
+}
+SEMAPHORES = (["lsnd", "lplc", "lx", "lgh", "st", "loc", "arr", "din", "pin", "win_in", "tcomb", "tdef"]
+              + ["c%d" % k for k in range(60)])
+
+_PLAN = {}
+
+
+def _bits(mask):
+    return [1 << i for i in range(16) if (mask >> i) & 1]
+
+
+def _count(mask):
+    return len(_bits(mask))
+
+
+def _plan(T, topo):
+    if _PLAN:
+        return _PLAN
+    cores = [int(c) for c in T.cores]
+    n = len(cores)
+    world = range(512)
+    send, relay, helper = {}, {}, {}
+    for r, a in enumerate(cores):
+        chip = [c for c in world if c != a and topo.host(c) == topo.host(a) and topo.chip(c) == topo.chip(a)]
+        halves = []
+        used = set()
+        for h in (0, 1):
+            b = cores[(r - 1) % n] if h == 0 else cores[(r + 1) % n]
+            cand = [c for c in chip if topo.may_write(c, b) and c not in used]
+            if not cand:
+                cand = [c for c in world if topo.same_plane(a, c) and topo.host(c) != topo.host(a)
+                        and topo.may_write(a, c) and topo.may_write(c, b)
+                        and any(topo.mates(c, m) and topo.chip(m) == topo.chip(b) for m in world)]
+            near = [c for c in cand if topo.die(c) == topo.die(a)][0]
+            far = [c for c in cand if topo.die(c) != topo.die(a)][0]
+            used.update((near, far))
+            crosses = topo.rack(topo.host(a)) != topo.rack(topo.host(b))
+            halves.append({"half": h, "dst": b, "relays": [near, far], "first": crosses,
+                           "near": topo.chip(near) == topo.chip(a) and topo.host(near) == topo.host(a)})
+        halves.sort(key=lambda d: not d["first"])
+        send[a] = halves
+        k = 0
+        for d in sorted(halves, key=lambda d: not d["near"]):
+            for j, c in enumerate(d["relays"]):
+                relay[c] = {"src": a, "dst": d["dst"], "table": k,
+                            "col": COLS + (CAP if d["half"] == 0 else 0) + j * PIECE}
+                k += 1
+        h = [c for c in chip if c not in used and topo.die(c) == topo.die(a)][0]
+        helper[h] = a
+    for a, halves in send.items():
+        for d in halves:
+            masks = []
+            for j, c in enumerate(d["relays"]):
+                m = 0
+                for b in _bits(topo.mask(a, c))[j::2]:
+                    m |= b
+                masks.append(m)
+                relay[c]["inc"] = _count(m)
+            d["masks"] = masks
+    _PLAN.update({"send": send, "relay": relay, "helper": helper})
+    return _PLAN
+
+
+def _seq(T):
+    n = [0]
+
+    def new():
+        n[0] += 1
+        return T.sem["c%d" % (n[0] - 1)]
+    return new
+
+
+def _ids(topo, dst, src):
+    rid, pid = topo.addr(dst, src)
+    return [DstId(rid=rid, pnc=pid)]
+
+
+def _put(g, T, topo, src, dst, out, in_, sem, mask):
+    rid, pid = topo.addr(dst, src)
+    g.remote_dma(out, in_, sem, T.sem.loc, pid, rid, mask)
+
+
+def _make_comb(g, T, new, out):
+    v = g.vector
+    a, b, c = new(), new(), new()
+    g.iota(T.combi[:, :], [[1, 144]], 0, 0).then_inc(a, 1)
+    v.wait_ge(a, 1)
+    v.tensor_scalar(T.comba[:, :], T.combi[:, :], 15, None, AluOpType.bitwise_and).then_inc(b, 1)
+    v.wait_ge(b, 1)
+    v.tensor_scalar(out, T.comba[:, :], 0, None, AluOpType.is_equal).then_inc(c, 1)
+    return c
+
+
+def _part_mod(g, T, new):
+    a, b = new(), new()
+    g.iota(T.pidx[:, :], [[0, 8]], 0, 1).then_inc(a, 1)
+    g.vector.wait_ge(a, 1)
+    g.vector.tensor_scalar(T.pmod[:, :], T.pidx[:, :], 15, None, AluOpType.bitwise_and).then_inc(b, 1)
+    g.vector.wait_ge(b, 1)
+
+
+def _make_def(g, T, new, c0, out):
+    v = g.vector
+    a, b, c = new(), new(), new()
+    g.iota(T.defi[:, :], [[16, TABC]], 16 * c0, 0, allow_small_or_imprecise_dtypes=True).then_inc(a, 1)
+    v.tensor_copy(T.pmf[:, :], T.pmod[:, :]).then_inc(b, 1)
+    v.wait_ge(a, 1)
+    v.wait_ge(b, 1)
+    v.tensor_scalar(out, T.defi[:, :], T.pmf[:, 0:1], None, AluOpType.add).then_inc(c, 1)
+    return c
+
+
+def _make_val_iotas(g, T, new):
+    a, b = new(), new()
+    g.iota(T.hi[:, :], [[0, 16], [0, 2], [256, 8]], COLS, 0, allow_small_or_imprecise_dtypes=True).then_inc(a, 1)
+    g.iota(T.lo[:, :], [[128, 16], [8, 2], [0, 8]], -1, 1, allow_small_or_imprecise_dtypes=True).then_inc(b, 1)
+    return a, b
+
+
+def _make_val(g, T, new, a, b):
+    v = g.vector
+    c, d, e, f, h = new(), new(), new(), new(), new()
+    v.tensor_scalar(T.is0[:, :], T.pmod[:, :], 0, None, AluOpType.is_equal).then_inc(c, 1)
+    v.tensor_scalar(T.is1[:, :], T.pmod[:, :], 1, 0.125, AluOpType.is_equal, AluOpType.mult).then_inc(d, 1)
+    v.wait_ge(a, 1)
+    v.wait_ge(c, 1)
+    v.tensor_scalar(T.him[:, :], T.hi[:, :], T.is0[:, 0:1], None, AluOpType.mult).then_inc(e, 1)
+    v.wait_ge(b, 1)
+    v.wait_ge(d, 1)
+    v.tensor_scalar(T.lom[:, :], T.lo[:, :], T.is1[:, 0:1], None, AluOpType.mult).then_inc(f, 1)
+    v.wait_ge(e, 1)
+    v.wait_ge(f, 1)
+    v.tensor_tensor(T.val[:, :], T.him[:, :], T.lom[:, :], AluOpType.add).then_inc(h, 1)
+    return h
+
+
+def _invert_scatter(g, T, new, ready):
+    v = g.vector
+    a, b = new(), new()
+    v.wait_ge(ready[0][0], ready[0][1])
+    v.tensor_copy(T.poff[:, :], T.plci[:, :]).then_inc(a, 1)
+
+    def scatter():
+        v.wait_ge(a, 1)
+        for s, n in ready[1:]:
+            v.wait_ge(s, n)
+        v.tensor_copy(T.win[:, 0:COLS].indirect(T.poff[:, 0:16]), T.val[:, :]).then_inc(b, 1)
+        return b
+    return scatter
+
+
+def _invert_matmul(g, T, new, c0, n):
+    a = new()
+    for q in range(16):
+        lo = 16 * c0 + q
+        mm = g.tensor.matmul(T.psw[:, 0:n], T.comb[:, 16 - q:144 - q], T.win[:, lo:16 * (c0 + n):16], q == 0, q == 15)
+        if q == 15:
+            mm.then_inc(a, 1)
+    return a
+
+
+def _rank(g, core, T, topo, plan):
+    new = _seq(T)
+    v, s, pe, sy = g.vector, g.scalar, g.tensor, g.sync
+    sem = T.sem
+    halves = plan["send"][core]
+    helper = [h for h, r in plan["helper"].items() if r == core][0]
+    sy.dma_start(T.sndi[:, :], T.snd[:, :]).then_inc(sem.lsnd, 16)
+    s.dma_start(T.plci[:, :], T.plc[:, :]).then_inc(sem.lplc, 16)
+    sy.dma_start(T.xs[:, :], T.x[:, :]).then_inc(sem.lx, 16)
+    sy.wait_ge(sem.lsnd, 16)
+    sy.dma_start(T.gat[:, 0:COLS], T.gh[:, :]).then_inc(sem.lgh, 16)
+
+    ri, ra, rr = new(), new(), new()
+    g.iota(T.repi[:, :], [[1, 128]], 0, -1).then_inc(ri, 1)
+    v.wait_ge(ri, 1)
+    v.tensor_scalar(T.repa[:, :], T.repi[:, :], 15, None, AluOpType.bitwise_and).then_inc(ra, 1)
+    v.wait_ge(ra, 1)
+    v.tensor_scalar(T.rep[:, :], T.repa[:, :], 0, None, AluOpType.is_equal).then_inc(rr, 1)
+    _part_mod(g, T, new)
+    a, b = _make_val_iotas(g, T, new)
+    val = _make_val(g, T, new, a, b)
+    zero = new()
+    v.memset(T.win[:, 0:16 * OWNC], 0.0).then_inc(zero, 1)
+
+    sf, sm, so = new(), new(), new()
+    v.wait_ge(sem.lsnd, 16)
+    v.tensor_copy(T.sndf[:, :], T.sndi[:, :]).then_inc(sf, 1)
+    pe.wait_ge(rr, 1)
+    pe.wait_ge(sf, 1)
+    pe.matmul(T.psa[:, 0:128], T.rep[:, :], T.sndf[:, :], True, True).then_inc(sm, 1)
+    scatter = _invert_scatter(g, T, new, [(sem.lplc, 16), (val, 1), (zero, 1)])
+    v.wait_ge(sm, 1)
+    v.tensor_copy(T.soff[:, :], T.psa[:, 0:128]).then_inc(so, 1)
+    sc = scatter()
+
+    g.wait_ge(sem.lplc, 16)
+    m = topo.mask(core, helper)
+    _put(g, T, topo, core, helper, T.plci[:, :], T.plci[:, :], sem.pin, m)
+    sent = _count(m)
+
+    pe.wait_ge(sc, 1)
+    pe.wait_ge(sem.tcomb, 8)
+    pw = _invert_matmul(g, T, new, 0, OWNC)
+
+    for q in (v, s):
+        q.wait_ge(so, 1)
+        q.wait_ge(sem.lx, 16)
+    for k, d in enumerate(halves):
+        done = []
+        for j in (0, 1):
+            c = (d["half"] * CAP + j * PIECE) // 16
+            src = T.xs[:, 0:COLS].indirect(T.soff[:, c:c + PC])
+            dst = T.stage[:, (2 * k + j) * PIECE:(2 * k + j + 1) * PIECE]
+            e = new()
+            if j == 0:
+                v.tensor_copy(dst, src).then_inc(e, 1)
+            else:
+                s.activation(dst, src, ActivationFunctionType.Copy, bias=-0.0).then_inc(e, 1)
+            done.append(e)
+        for e in done:
+            g.wait_ge(e, 1)
+        tr = []
+        for j, c in enumerate(d["relays"]):
+            tr.append(RemoteDMATransfer(dst_ids=_ids(topo, c, core), dma_engine_mask=d["masks"][j], remote_sem=sem.din,
+                                        src=T.stage[:, (2 * k + j) * PIECE:(2 * k + j + 1) * PIECE], dst=T.hop[:, :]))
+            sent += _count(d["masks"][j])
+        g.remote_dma_fused(tr, local_sem=sem.loc)
+
+    wa, wb = new(), new()
+    v.wait_ge(pw, 1)
+    v.wait_ge(sem.tdef, 24)
+    v.tensor_tensor(T.wf[:, :], T.psw[:, 0:OWNC], T.plcdef[:, :], AluOpType.max).then_inc(wa, 1)
+    v.wait_ge(wa, 1)
+    v.tensor_copy(T.wm[:, :], T.wf[:, :]).then_inc(wb, 1)
+
+    for q in (v, s):
+        q.wait_ge(wb, 1)
+        q.wait_ge(sem.lgh, 16)
+        q.wait_ge(sem.arr, 32)
+    chunks = []
+    for i in range(4):
+        for j in (0, 1):
+            if i < 3:
+                c = (3 * j + i) * PC
+                col, off = 16 * c, T.wm[:, c:c + PC]
+            else:
+                col, off = 16 * (OWNC + j * PC), T.wh[:, j * PC:(j + 1) * PC]
+                (v, s)[j].wait_ge(sem.win_in, 8)
+            src = T.gat[:, :].indirect(off)
+            dst = T.ys[:, col:col + PIECE]
+            e = new()
+            if j == 0:
+                v.tensor_copy(dst, src).then_inc(e, 1)
+            else:
+                s.activation(dst, src, ActivationFunctionType.Copy, bias=-0.0).then_inc(e, 1)
+            chunks.append((e, col))
+    for i, (e, col) in enumerate(chunks):
+        q = s if i == 7 else sy
+        q.wait_ge(e, 1)
+        q.dma_start(T.y[:, col:col + PIECE], T.ys[:, col:col + PIECE]).then_inc(sem.st, 16)
+    sy.wait_ge(sem.st, 128)
+    g.wait_ge(sem.loc, sent)
+
+
+def _relay(g, core, T, topo, job):
+    new = _seq(T)
+    sem = T.sem
+    m = topo.mask(core, job["dst"])
+    k = job["table"]
+    if k == 0:
+        e = _make_comb(g, T, new, T.combs[:, :])
+        g.wait_ge(e, 1)
+        _put(g, T, topo, core, job["src"], T.comb[:, :], T.combs[:, :], sem.tcomb, m)
+    else:
+        c0 = (k - 1) * TABC
+        _part_mod(g, T, new)
+        e = _make_def(g, T, new, c0, T.defs[:, :])
+        g.wait_ge(e, 1)
+        _put(g, T, topo, core, job["src"], T.plcdef[:, c0:c0 + TABC], T.defs[:, :], sem.tdef, m)
+    g.wait_ge(sem.din, job["inc"])
+    _put(g, T, topo, core, job["dst"], T.gat[:, job["col"]:job["col"] + PIECE], T.hop[:, :], sem.arr, m)
+    g.wait_ge(sem.loc, 2 * _count(m))
+
+
+def _helper(g, core, T, topo, rank):
+    new = _seq(T)
+    v = g.vector
+    sem = T.sem
+    _part_mod(g, T, new)
+    a, b = _make_val_iotas(g, T, new)
+    val = _make_val(g, T, new, a, b)
+    zero = new()
+    v.memset(T.win[:, 16 * OWNC:COLS], 0.0).then_inc(zero, 1)
+    comb = _make_comb(g, T, new, T.comb[:, :])
+    dfl = _make_def(g, T, new, OWNC, T.defs[:, :])
+    src_n = _count(topo.mask(rank, core))
+    sc = _invert_scatter(g, T, new, [(sem.pin, src_n), (val, 1), (zero, 1)])()
+    g.tensor.wait_ge(comb, 1)
+    g.tensor.wait_ge(sc, 1)
+    pw = _invert_matmul(g, T, new, OWNC, TABC)
+    wa, wb = new(), new()
+    v.wait_ge(pw, 1)
+    v.wait_ge(dfl, 1)
+    v.tensor_tensor(T.wf[:, 0:TABC], T.psw[:, 0:TABC], T.defs[:, :], AluOpType.max).then_inc(wa, 1)
+    v.wait_ge(wa, 1)
+    v.tensor_copy(T.wl[:, :], T.wf[:, 0:TABC]).then_inc(wb, 1)
+    g.wait_ge(wb, 1)
+    m = 0
+    for bit in _bits(topo.mask(core, rank))[::2]:
+        m |= bit
+    _put(g, T, topo, core, rank, T.wh[:, :], T.wl[:, :], sem.win_in, m)
+    g.wait_ge(sem.loc, _count(m))
+
+
+def rank_program(g, core, T, topo):
+    plan = _plan(T, topo)
+    if core in plan["send"]:
+        _rank(g, core, T, topo, plan)
+    elif core in plan["relay"]:
+        _relay(g, core, T, topo, plan["relay"][core])
+    elif core in plan["helper"]:
+        _helper(g, core, T, topo, plan["helper"][core])

@@ -7,6 +7,8 @@ PIECE = 512
 PC = PIECE // 16
 OWNC = 192
 TABC = 64
+GH1 = 2048
+CHUNKS = [256, 512, 512, 512, 256]
 
 SCRATCH = {
     "sndi": ("sbuf", [16, 128], "int32"),
@@ -47,7 +49,7 @@ SCRATCH = {
     "psa": ("psum", [128, 512], "float32"),
     "psw": ("psum", [128, 512], "float32"),
 }
-SEMAPHORES = (["lsnd", "lplc", "lx", "lgh", "st", "loc", "arr", "din", "pin", "win_in", "tcomb", "tdef"]
+SEMAPHORES = (["lsnd", "lplc", "lx", "lgh", "st", "loc", "arr", "din", "pin", "win_in", "tcomb", "tdef", "sentb"]
               + ["c%d" % k for k in range(60)])
 
 _PLAN = {}
@@ -165,7 +167,7 @@ def _make_val_iotas(g, T, new):
     return a, b
 
 
-def _make_val(g, T, new, a, b):
+def _make_val(g, T, new, a, b, between=None):
     v = g.vector
     c, d, e, f, h = new(), new(), new(), new(), new()
     v.tensor_scalar(T.is0[:, :], T.pmod[:, :], 0, None, AluOpType.is_equal).then_inc(c, 1)
@@ -173,6 +175,8 @@ def _make_val(g, T, new, a, b):
     v.wait_ge(a, 1)
     v.wait_ge(c, 1)
     v.tensor_scalar(T.him[:, :], T.hi[:, :], T.is0[:, 0:1], None, AluOpType.mult).then_inc(e, 1)
+    if between is not None:
+        between()
     v.wait_ge(b, 1)
     v.wait_ge(d, 1)
     v.tensor_scalar(T.lom[:, :], T.lo[:, :], T.is1[:, 0:1], None, AluOpType.mult).then_inc(f, 1)
@@ -182,19 +186,16 @@ def _make_val(g, T, new, a, b):
     return h
 
 
-def _invert_scatter(g, T, new, ready):
+def _invert_scatter(g, T, new, plc, ready):
     v = g.vector
     a, b = new(), new()
-    v.wait_ge(ready[0][0], ready[0][1])
+    v.wait_ge(plc[0], plc[1])
     v.tensor_copy(T.poff[:, :], T.plci[:, :]).then_inc(a, 1)
-
-    def scatter():
-        v.wait_ge(a, 1)
-        for s, n in ready[1:]:
-            v.wait_ge(s, n)
-        v.tensor_copy(T.win[:, 0:COLS].indirect(T.poff[:, 0:16]), T.val[:, :]).then_inc(b, 1)
-        return b
-    return scatter
+    v.wait_ge(a, 1)
+    for s in ready:
+        v.wait_ge(s, 1)
+    v.tensor_copy(T.win[:, 0:COLS].indirect(T.poff[:, 0:16]), T.val[:, :]).then_inc(b, 1)
+    return b
 
 
 def _invert_matmul(g, T, new, c0, n):
@@ -217,8 +218,12 @@ def _rank(g, core, T, topo, plan):
     s.dma_start(T.plci[:, :], T.plc[:, :]).then_inc(sem.lplc, 16)
     sy.dma_start(T.xs[:, :], T.x[:, :]).then_inc(sem.lx, 16)
     sy.wait_ge(sem.lsnd, 16)
-    sy.dma_start(T.gat[:, 0:COLS], T.gh[:, :]).then_inc(sem.lgh, 16)
+    sy.dma_start(T.gat[:, 0:GH1], T.gh[:, 0:GH1]).then_inc(sem.lgh, 16)
+    sy.wait_ge(sem.sentb, 1)
+    sy.dma_start(T.gat[:, GH1:COLS], T.gh[:, GH1:COLS]).then_inc(sem.lgh, 16)
 
+    zero = new()
+    v.memset(T.win[:, 0:16 * OWNC], 0.0).then_inc(zero, 1)
     ri, ra, rr = new(), new(), new()
     g.iota(T.repi[:, :], [[1, 128]], 0, -1).then_inc(ri, 1)
     v.wait_ge(ri, 1)
@@ -227,20 +232,19 @@ def _rank(g, core, T, topo, plan):
     v.tensor_scalar(T.rep[:, :], T.repa[:, :], 0, None, AluOpType.is_equal).then_inc(rr, 1)
     _part_mod(g, T, new)
     a, b = _make_val_iotas(g, T, new)
-    val = _make_val(g, T, new, a, b)
-    zero = new()
-    v.memset(T.win[:, 0:16 * OWNC], 0.0).then_inc(zero, 1)
 
     sf, sm, so = new(), new(), new()
-    v.wait_ge(sem.lsnd, 16)
-    v.tensor_copy(T.sndf[:, :], T.sndi[:, :]).then_inc(sf, 1)
+
+    def snd_float():
+        v.wait_ge(sem.lsnd, 16)
+        v.tensor_copy(T.sndf[:, :], T.sndi[:, :]).then_inc(sf, 1)
+    val = _make_val(g, T, new, a, b, snd_float)
     pe.wait_ge(rr, 1)
     pe.wait_ge(sf, 1)
     pe.matmul(T.psa[:, 0:128], T.rep[:, :], T.sndf[:, :], True, True).then_inc(sm, 1)
-    scatter = _invert_scatter(g, T, new, [(sem.lplc, 16), (val, 1), (zero, 1)])
     v.wait_ge(sm, 1)
     v.tensor_copy(T.soff[:, :], T.psa[:, 0:128]).then_inc(so, 1)
-    sc = scatter()
+    sc = _invert_scatter(g, T, new, (sem.lplc, 16), [val, zero])
 
     g.wait_ge(sem.lplc, 16)
     m = topo.mask(core, helper)
@@ -274,6 +278,7 @@ def _rank(g, core, T, topo, plan):
                                         src=T.stage[:, (2 * k + j) * PIECE:(2 * k + j + 1) * PIECE], dst=T.hop[:, :]))
             sent += _count(d["masks"][j])
         g.remote_dma_fused(tr, local_sem=sem.loc)
+    g.sem_inc(sem.sentb, 1)
 
     wa, wb = new(), new()
     v.wait_ge(pw, 1)
@@ -284,30 +289,35 @@ def _rank(g, core, T, topo, plan):
 
     for q in (v, s):
         q.wait_ge(wb, 1)
-        q.wait_ge(sem.lgh, 16)
+        q.wait_ge(sem.lgh, 32)
         q.wait_ge(sem.arr, 32)
-    chunks = []
-    for i in range(4):
+    col = 0
+    helped = [False, False]
+    for w in CHUNKS:
+        done = []
         for j in (0, 1):
-            if i < 3:
-                c = (3 * j + i) * PC
-                col, off = 16 * c, T.wm[:, c:c + PC]
+            a = col + j * w
+            c = a // 16
+            if c < OWNC:
+                off = T.wm[:, c:c + w // 16]
             else:
-                col, off = 16 * (OWNC + j * PC), T.wh[:, j * PC:(j + 1) * PC]
-                (v, s)[j].wait_ge(sem.win_in, 8)
+                off = T.wh[:, c - OWNC:c - OWNC + w // 16]
+                if not helped[j]:
+                    (v, s)[j].wait_ge(sem.win_in, 8)
+                    helped[j] = True
             src = T.gat[:, :].indirect(off)
-            dst = T.ys[:, col:col + PIECE]
+            dst = T.ys[:, a:a + w]
             e = new()
             if j == 0:
                 v.tensor_copy(dst, src).then_inc(e, 1)
             else:
                 s.activation(dst, src, ActivationFunctionType.Copy, bias=-0.0).then_inc(e, 1)
-            chunks.append((e, col))
-    for i, (e, col) in enumerate(chunks):
-        q = s if i == 7 else sy
-        q.wait_ge(e, 1)
-        q.dma_start(T.y[:, col:col + PIECE], T.ys[:, col:col + PIECE]).then_inc(sem.st, 16)
-    sy.wait_ge(sem.st, 128)
+            done.append(e)
+        for e in done:
+            sy.wait_ge(e, 1)
+        sy.dma_start(T.y[:, col:col + 2 * w], T.ys[:, col:col + 2 * w]).then_inc(sem.st, 16)
+        col += 2 * w
+    sy.wait_ge(sem.st, 16 * len(CHUNKS))
     g.wait_ge(sem.loc, sent)
 
 
@@ -335,15 +345,14 @@ def _helper(g, core, T, topo, rank):
     new = _seq(T)
     v = g.vector
     sem = T.sem
+    zero = new()
+    v.memset(T.win[:, 16 * OWNC:COLS], 0.0).then_inc(zero, 1)
     _part_mod(g, T, new)
     a, b = _make_val_iotas(g, T, new)
     val = _make_val(g, T, new, a, b)
-    zero = new()
-    v.memset(T.win[:, 16 * OWNC:COLS], 0.0).then_inc(zero, 1)
     comb = _make_comb(g, T, new, T.comb[:, :])
     dfl = _make_def(g, T, new, OWNC, T.defs[:, :])
-    src_n = _count(topo.mask(rank, core))
-    sc = _invert_scatter(g, T, new, [(sem.pin, src_n), (val, 1), (zero, 1)])()
+    sc = _invert_scatter(g, T, new, (sem.pin, _count(topo.mask(rank, core))), [val, zero])
     g.tensor.wait_ge(comb, 1)
     g.tensor.wait_ge(sc, 1)
     pw = _invert_matmul(g, T, new, OWNC, TABC)

@@ -167,7 +167,7 @@ def _make_val_iotas(g, T, new):
     return a, b
 
 
-def _make_val(g, T, new, a, b, between=None):
+def _make_val(g, T, new, a, b):
     v = g.vector
     c, d, e, f, h = new(), new(), new(), new(), new()
     v.tensor_scalar(T.is0[:, :], T.pmod[:, :], 0, None, AluOpType.is_equal).then_inc(c, 1)
@@ -175,8 +175,6 @@ def _make_val(g, T, new, a, b, between=None):
     v.wait_ge(a, 1)
     v.wait_ge(c, 1)
     v.tensor_scalar(T.him[:, :], T.hi[:, :], T.is0[:, 0:1], None, AluOpType.mult).then_inc(e, 1)
-    if between is not None:
-        between()
     v.wait_ge(b, 1)
     v.wait_ge(d, 1)
     v.tensor_scalar(T.lom[:, :], T.lo[:, :], T.is1[:, 0:1], None, AluOpType.mult).then_inc(f, 1)
@@ -230,30 +228,23 @@ def _rank(g, core, T, topo, plan):
     v.tensor_scalar(T.repa[:, :], T.repi[:, :], 15, None, AluOpType.bitwise_and).then_inc(ra, 1)
     v.wait_ge(ra, 1)
     v.tensor_scalar(T.rep[:, :], T.repa[:, :], 0, None, AluOpType.is_equal).then_inc(rr, 1)
-    _part_mod(g, T, new)
-    a, b = _make_val_iotas(g, T, new)
 
     sf, sm, so = new(), new(), new()
-
-    def snd_float():
-        v.wait_ge(sem.lsnd, 16)
-        v.tensor_copy(T.sndf[:, :], T.sndi[:, :]).then_inc(sf, 1)
-    val = _make_val(g, T, new, a, b, snd_float)
+    v.wait_ge(sem.lsnd, 16)
+    v.tensor_copy(T.sndf[:, :], T.sndi[:, :]).then_inc(sf, 1)
     pe.wait_ge(rr, 1)
     pe.wait_ge(sf, 1)
     pe.matmul(T.psa[:, 0:128], T.rep[:, :], T.sndf[:, :], True, True).then_inc(sm, 1)
     v.wait_ge(sm, 1)
     v.tensor_copy(T.soff[:, :], T.psa[:, 0:128]).then_inc(so, 1)
-    sc = _invert_scatter(g, T, new, (sem.lplc, 16), [val, zero])
 
+    pidx = new()
+    g.iota(T.pidx[:, :], [[0, 8]], 0, 1).then_inc(pidx, 1)
+    a, b = _make_val_iotas(g, T, new)
     g.wait_ge(sem.lplc, 16)
     m = topo.mask(core, helper)
     _put(g, T, topo, core, helper, T.plci[:, :], T.plci[:, :], sem.pin, m)
     sent = _count(m)
-
-    pe.wait_ge(sc, 1)
-    pe.wait_ge(sem.tcomb, 8)
-    pw = _invert_matmul(g, T, new, 0, OWNC)
 
     for q in (v, s):
         q.wait_ge(so, 1)
@@ -280,6 +271,15 @@ def _rank(g, core, T, topo, plan):
         g.remote_dma_fused(tr, local_sem=sem.loc)
     g.sem_inc(sem.sentb, 1)
 
+    pm = new()
+    v.wait_ge(pidx, 1)
+    v.tensor_scalar(T.pmod[:, :], T.pidx[:, :], 15, None, AluOpType.bitwise_and).then_inc(pm, 1)
+    v.wait_ge(pm, 1)
+    val = _make_val(g, T, new, a, b)
+    sc = _invert_scatter(g, T, new, (sem.lplc, 16), [val, zero])
+    pe.wait_ge(sc, 1)
+    pe.wait_ge(sem.tcomb, 8)
+    pw = _invert_matmul(g, T, new, 0, OWNC)
     wa, wb = new(), new()
     v.wait_ge(pw, 1)
     v.wait_ge(sem.tdef, 24)

@@ -4,10 +4,11 @@ from concourse.mybir import AluOpType, ActivationFunctionType
 COLS = 4096
 CAP = 1024
 PIECE = 512
-PC = PIECE // 16
-OWNC = 192
+HALF = PIECE // 32
+OWNC = 128
 TABC = 64
-GH1 = 2048
+HELPERS = 2
+GH1 = 1280
 CHUNKS = [256, 512, 512, 512, 256]
 
 SCRATCH = {
@@ -21,8 +22,9 @@ SCRATCH = {
     "stage": ("sbuf", [128, 2048], "bfloat16"),
     "gat": ("sbuf", [128, 6144], "bfloat16"),
     "ys": ("sbuf", [128, 4096], "bfloat16"),
-    "wm": ("sbuf", [128, 192], "uint16"),
-    "wh": ("sbuf", [128, 64], "uint16"),
+    "wm": ("sbuf", [128, 128], "uint16"),
+    "wh": ("sbuf", [128, 128], "uint16"),
+    "plcd": ("dram", [128, 16], "int32"),
     "plci": ("sbuf", [128, 16], "int32"),
     "poff": ("sbuf", [128, 16], "uint16"),
     "win": ("sbuf", [128, 4096], "bfloat16"),
@@ -36,10 +38,11 @@ SCRATCH = {
     "pmf": ("sbuf", [128, 8], "float32"),
     "is0": ("sbuf", [128, 8], "float32"),
     "is1": ("sbuf", [128, 8], "float32"),
-    "wf": ("sbuf", [128, 192], "float32"),
+    "wf": ("sbuf", [128, 128], "float32"),
     "wl": ("sbuf", [128, 64], "uint16"),
     "comb": ("sbuf", [128, 144], "bfloat16"),
-    "plcdef": ("sbuf", [128, 192], "float32"),
+    "plcdef": ("sbuf", [128, 128], "float32"),
+    "vals": ("sbuf", [128, 256], "bfloat16"),
     "combi": ("sbuf", [128, 144], "int32"),
     "comba": ("sbuf", [128, 144], "int32"),
     "combs": ("sbuf", [128, 144], "bfloat16"),
@@ -49,8 +52,8 @@ SCRATCH = {
     "psa": ("psum", [128, 512], "float32"),
     "psw": ("psum", [128, 512], "float32"),
 }
-SEMAPHORES = (["lsnd", "lplc", "lx", "lgh", "st", "loc", "arr", "din", "pin", "win_in", "tcomb", "tdef", "sentb"]
-              + ["c%d" % k for k in range(60)])
+SEMAPHORES = (["lsnd", "lplc", "ltile", "lx", "lgh", "st", "loc", "arr", "din", "pin", "win0", "win1",
+               "tcomb", "tval", "tdef", "sentb"] + ["c%d" % k for k in range(60)])
 
 _PLAN = {}
 
@@ -84,29 +87,36 @@ def _plan(T, topo):
             near = [c for c in cand if topo.die(c) == topo.die(a)][0]
             far = [c for c in cand if topo.die(c) != topo.die(a)][0]
             used.update((near, far))
-            crosses = topo.rack(topo.host(a)) != topo.rack(topo.host(b))
-            halves.append({"half": h, "dst": b, "relays": [near, far], "first": crosses,
-                           "near": topo.chip(near) == topo.chip(a) and topo.host(near) == topo.host(a)})
+            halves.append({"half": h, "dst": b, "relays": [near, far],
+                           "first": topo.rack(topo.host(a)) != topo.rack(topo.host(b)), "near": near in chip})
         halves.sort(key=lambda d: not d["first"])
-        send[a] = halves
         k = 0
         for d in sorted(halves, key=lambda d: not d["near"]):
+            d["pieces"] = []
             for j, c in enumerate(d["relays"]):
                 relay[c] = {"src": a, "dst": d["dst"], "table": k,
                             "col": COLS + (CAP if d["half"] == 0 else 0) + j * PIECE}
+                d["pieces"].insert(0, {"relay": c, "off": (d["half"] * CAP + j * PIECE) // 16, "mask": topo.mask(a, c)})
                 k += 1
-        h = [c for c in chip if c not in used and topo.die(c) == topo.die(a)][0]
-        helper[h] = a
-    for a, halves in send.items():
+        away = 0
         for d in halves:
-            masks = []
-            for j, c in enumerate(d["relays"]):
-                m = 0
-                for b in _bits(topo.mask(a, c))[j::2]:
-                    m |= b
-                masks.append(m)
-                relay[c]["inc"] = _count(m)
-            d["masks"] = masks
+            if not d["near"]:
+                for p in d["pieces"]:
+                    away |= p["mask"]
+        if away:
+            order = [p for pair in zip(*[d["pieces"] for d in halves]) for p in pair]
+            for d in halves:
+                if d["near"]:
+                    for p in d["pieces"]:
+                        p["mask"] &= ~away
+        else:
+            order = [p for d in halves for p in d["pieces"]]
+        for p in order:
+            relay[p["relay"]]["inc"] = _count(p["mask"])
+        send[a] = order
+        rest = sorted([c for c in chip if c not in used], key=lambda c: topo.die(c) != topo.die(a))
+        for k in range(HELPERS):
+            helper[rest[k]] = (a, k)
     _PLAN.update({"send": send, "relay": relay, "helper": helper})
     return _PLAN
 
@@ -167,7 +177,7 @@ def _make_val_iotas(g, T, new):
     return a, b
 
 
-def _make_val(g, T, new, a, b):
+def _make_val(g, T, new, a, b, out):
     v = g.vector
     c, d, e, f, h = new(), new(), new(), new(), new()
     v.tensor_scalar(T.is0[:, :], T.pmod[:, :], 0, None, AluOpType.is_equal).then_inc(c, 1)
@@ -180,7 +190,7 @@ def _make_val(g, T, new, a, b):
     v.tensor_scalar(T.lom[:, :], T.lo[:, :], T.is1[:, 0:1], None, AluOpType.mult).then_inc(f, 1)
     v.wait_ge(e, 1)
     v.wait_ge(f, 1)
-    v.tensor_tensor(T.val[:, :], T.him[:, :], T.lom[:, :], AluOpType.add).then_inc(h, 1)
+    v.tensor_tensor(out, T.him[:, :], T.lom[:, :], AluOpType.add).then_inc(h, 1)
     return h
 
 
@@ -190,8 +200,8 @@ def _invert_scatter(g, T, new, plc, ready):
     v.wait_ge(plc[0], plc[1])
     v.tensor_copy(T.poff[:, :], T.plci[:, :]).then_inc(a, 1)
     v.wait_ge(a, 1)
-    for s in ready:
-        v.wait_ge(s, 1)
+    for s, n in ready:
+        v.wait_ge(s, n)
     v.tensor_copy(T.win[:, 0:COLS].indirect(T.poff[:, 0:16]), T.val[:, :]).then_inc(b, 1)
     return b
 
@@ -206,16 +216,27 @@ def _invert_matmul(g, T, new, c0, n):
     return a
 
 
+def _helpers(plan, rank):
+    return sorted([h for h in plan["helper"] if plan["helper"][h][0] == rank], key=lambda h: plan["helper"][h][1])
+
+
+def _plc_mask(topo, rank, helpers):
+    m = topo.mask(rank, helpers[0])
+    for h in helpers[1:]:
+        m &= topo.mask(rank, h)
+    return m
+
+
 def _rank(g, core, T, topo, plan):
     new = _seq(T)
     v, s, pe, sy = g.vector, g.scalar, g.tensor, g.sync
     sem = T.sem
-    halves = plan["send"][core]
-    helper = [h for h, r in plan["helper"].items() if r == core][0]
+    helpers = _helpers(plan, core)
     sy.dma_start(T.sndi[:, :], T.snd[:, :]).then_inc(sem.lsnd, 16)
-    s.dma_start(T.plci[:, :], T.plc[:, :]).then_inc(sem.lplc, 16)
+    s.dma_start(T.plcd[:, :], T.plc[:, :]).then_inc(sem.lplc, 16)
     sy.dma_start(T.xs[:, :], T.x[:, :]).then_inc(sem.lx, 16)
     sy.wait_ge(sem.lsnd, 16)
+    sy.dma_start(T.plci[:, :], T.plc[:, :]).then_inc(sem.ltile, 16)
     sy.dma_start(T.gat[:, 0:GH1], T.gh[:, 0:GH1]).then_inc(sem.lgh, 16)
     sy.wait_ge(sem.sentb, 1)
     sy.dma_start(T.gat[:, GH1:COLS], T.gh[:, GH1:COLS]).then_inc(sem.lgh, 16)
@@ -238,23 +259,23 @@ def _rank(g, core, T, topo, plan):
     v.wait_ge(sm, 1)
     v.tensor_copy(T.soff[:, :], T.psa[:, 0:128]).then_inc(so, 1)
 
-    pidx = new()
-    g.iota(T.pidx[:, :], [[0, 8]], 0, 1).then_inc(pidx, 1)
-    a, b = _make_val_iotas(g, T, new)
     g.wait_ge(sem.lplc, 16)
-    m = topo.mask(core, helper)
-    _put(g, T, topo, core, helper, T.plci[:, :], T.plci[:, :], sem.pin, m)
+    m = _plc_mask(topo, core, helpers)
+    g.remote_dma_fused([RemoteDMATransfer(dst_ids=[d for h in helpers for d in _ids(topo, h, core)], dma_engine_mask=m,
+                                          remote_sem=sem.pin, srcs=[T.plcd[:, :]], dsts=[T.plci[:, :] for h in helpers])],
+                       local_sem=sem.loc)
     sent = _count(m)
 
     for q in (v, s):
         q.wait_ge(so, 1)
         q.wait_ge(sem.lx, 16)
-    for k, d in enumerate(halves):
+    for k, p in enumerate(plan["send"][core]):
         done = []
         for j in (0, 1):
-            c = (d["half"] * CAP + j * PIECE) // 16
-            src = T.xs[:, 0:COLS].indirect(T.soff[:, c:c + PC])
-            dst = T.stage[:, (2 * k + j) * PIECE:(2 * k + j + 1) * PIECE]
+            c = p["off"] + j * HALF
+            src = T.xs[:, 0:COLS].indirect(T.soff[:, c:c + HALF])
+            lo = k * PIECE + j * PIECE // 2
+            dst = T.stage[:, lo:lo + PIECE // 2]
             e = new()
             if j == 0:
                 v.tensor_copy(dst, src).then_inc(e, 1)
@@ -263,26 +284,17 @@ def _rank(g, core, T, topo, plan):
             done.append(e)
         for e in done:
             g.wait_ge(e, 1)
-        tr = []
-        for j, c in enumerate(d["relays"]):
-            tr.append(RemoteDMATransfer(dst_ids=_ids(topo, c, core), dma_engine_mask=d["masks"][j], remote_sem=sem.din,
-                                        src=T.stage[:, (2 * k + j) * PIECE:(2 * k + j + 1) * PIECE], dst=T.hop[:, :]))
-            sent += _count(d["masks"][j])
-        g.remote_dma_fused(tr, local_sem=sem.loc)
+        _put(g, T, topo, core, p["relay"], T.hop[:, :], T.stage[:, k * PIECE:(k + 1) * PIECE], sem.din, p["mask"])
+        sent += _count(p["mask"])
     g.sem_inc(sem.sentb, 1)
 
-    pm = new()
-    v.wait_ge(pidx, 1)
-    v.tensor_scalar(T.pmod[:, :], T.pidx[:, :], 15, None, AluOpType.bitwise_and).then_inc(pm, 1)
-    v.wait_ge(pm, 1)
-    val = _make_val(g, T, new, a, b)
-    sc = _invert_scatter(g, T, new, (sem.lplc, 16), [val, zero])
+    sc = _invert_scatter(g, T, new, (sem.ltile, 16), [(sem.tval, 8), (zero, 1)])
     pe.wait_ge(sc, 1)
     pe.wait_ge(sem.tcomb, 8)
     pw = _invert_matmul(g, T, new, 0, OWNC)
     wa, wb = new(), new()
     v.wait_ge(pw, 1)
-    v.wait_ge(sem.tdef, 24)
+    v.wait_ge(sem.tdef, 16)
     v.tensor_tensor(T.wf[:, :], T.psw[:, 0:OWNC], T.plcdef[:, :], AluOpType.max).then_inc(wa, 1)
     v.wait_ge(wa, 1)
     v.tensor_copy(T.wm[:, :], T.wf[:, :]).then_inc(wb, 1)
@@ -292,7 +304,7 @@ def _rank(g, core, T, topo, plan):
         q.wait_ge(sem.lgh, 32)
         q.wait_ge(sem.arr, 32)
     col = 0
-    helped = [False, False]
+    came = [set(), set()]
     for w in CHUNKS:
         done = []
         for j in (0, 1):
@@ -301,10 +313,12 @@ def _rank(g, core, T, topo, plan):
             if c < OWNC:
                 off = T.wm[:, c:c + w // 16]
             else:
-                off = T.wh[:, c - OWNC:c - OWNC + w // 16]
-                if not helped[j]:
-                    (v, s)[j].wait_ge(sem.win_in, 8)
-                    helped[j] = True
+                c -= OWNC
+                off = T.wh[:, c:c + w // 16]
+                k = c // TABC
+                if k not in came[j]:
+                    (v, s)[j].wait_ge(sem["win%d" % k], 8)
+                    came[j].add(k)
             src = T.gat[:, :].indirect(off)
             dst = T.ys[:, a:a + w]
             e = new()
@@ -327,11 +341,17 @@ def _relay(g, core, T, topo, job):
     m = topo.mask(core, job["dst"])
     k = job["table"]
     if k == 0:
+        a, b = _make_val_iotas(g, T, new)
+        _part_mod(g, T, new)
+        e = _make_val(g, T, new, a, b, T.vals[:, :])
+        g.wait_ge(e, 1)
+        _put(g, T, topo, core, job["src"], T.val[:, :], T.vals[:, :], sem.tval, m)
+    elif k == 1:
         e = _make_comb(g, T, new, T.combs[:, :])
         g.wait_ge(e, 1)
         _put(g, T, topo, core, job["src"], T.comb[:, :], T.combs[:, :], sem.tcomb, m)
     else:
-        c0 = (k - 1) * TABC
+        c0 = (k - 2) * TABC
         _part_mod(g, T, new)
         e = _make_def(g, T, new, c0, T.defs[:, :])
         g.wait_ge(e, 1)
@@ -341,21 +361,24 @@ def _relay(g, core, T, topo, job):
     g.wait_ge(sem.loc, 2 * _count(m))
 
 
-def _helper(g, core, T, topo, rank):
+def _helper(g, core, T, topo, plan):
     new = _seq(T)
     v = g.vector
     sem = T.sem
+    rank, k = plan["helper"][core]
+    c0 = OWNC + k * TABC
     zero = new()
-    v.memset(T.win[:, 16 * OWNC:COLS], 0.0).then_inc(zero, 1)
-    _part_mod(g, T, new)
+    v.memset(T.win[:, 16 * c0:16 * (c0 + TABC)], 0.0).then_inc(zero, 1)
     a, b = _make_val_iotas(g, T, new)
-    val = _make_val(g, T, new, a, b)
+    _part_mod(g, T, new)
+    val = _make_val(g, T, new, a, b, T.val[:, :])
     comb = _make_comb(g, T, new, T.comb[:, :])
-    dfl = _make_def(g, T, new, OWNC, T.defs[:, :])
-    sc = _invert_scatter(g, T, new, (sem.pin, _count(topo.mask(rank, core))), [val, zero])
+    dfl = _make_def(g, T, new, c0, T.defs[:, :])
+    n = _count(_plc_mask(topo, rank, _helpers(plan, rank)))
+    sc = _invert_scatter(g, T, new, (sem.pin, n), [(val, 1), (zero, 1)])
     g.tensor.wait_ge(comb, 1)
     g.tensor.wait_ge(sc, 1)
-    pw = _invert_matmul(g, T, new, OWNC, TABC)
+    pw = _invert_matmul(g, T, new, c0, TABC)
     wa, wb = new(), new()
     v.wait_ge(pw, 1)
     v.wait_ge(dfl, 1)
@@ -366,7 +389,7 @@ def _helper(g, core, T, topo, rank):
     m = 0
     for bit in _bits(topo.mask(core, rank))[::2]:
         m |= bit
-    _put(g, T, topo, core, rank, T.wh[:, :], T.wl[:, :], sem.win_in, m)
+    _put(g, T, topo, core, rank, T.wh[:, k * TABC:(k + 1) * TABC], T.wl[:, :], sem["win%d" % k], m)
     g.wait_ge(sem.loc, _count(m))
 
 
@@ -377,4 +400,4 @@ def rank_program(g, core, T, topo):
     elif core in plan["relay"]:
         _relay(g, core, T, topo, plan["relay"][core])
     elif core in plan["helper"]:
-        _helper(g, core, T, topo, plan["helper"][core])
+        _helper(g, core, T, topo, plan)

@@ -3,12 +3,11 @@ from concourse.mybir import AluOpType, ActivationFunctionType
 
 COLS = 4096
 CAP = 1024
-PIECE = 512
-HALF = PIECE // 32
+PART = 512
 OWNC = 128
 TABC = 64
 HELPERS = 2
-GH1 = 1280
+GH1 = 512
 CHUNKS = [256, 512, 512, 512, 256]
 
 SCRATCH = {
@@ -52,7 +51,7 @@ SCRATCH = {
     "psa": ("psum", [128, 512], "float32"),
     "psw": ("psum", [128, 512], "float32"),
 }
-SEMAPHORES = (["lsnd", "lplc", "ltile", "lx", "lgh", "st", "loc", "arr", "din", "pin", "win0", "win1",
+SEMAPHORES = (["lsnd", "lplc", "ltile", "lx", "lgh", "st", "loc", "arr", "din0", "din1", "pin", "win0", "win1",
                "tcomb", "tval", "tdef", "sentb"] + ["c%d" % k for k in range(60)])
 
 _PLAN = {}
@@ -72,7 +71,7 @@ def _plan(T, topo):
     cores = [int(c) for c in T.cores]
     n = len(cores)
     world = range(512)
-    send, relay, helper = {}, {}, {}
+    send, relay, helper, came = {}, {}, {}, {}
     for r, a in enumerate(cores):
         chip = [c for c in world if c != a and topo.host(c) == topo.host(a) and topo.chip(c) == topo.chip(a)]
         halves = []
@@ -93,31 +92,40 @@ def _plan(T, topo):
         k = 0
         for d in sorted(halves, key=lambda d: not d["near"]):
             d["pieces"] = []
+            cuts = 2 if d["first"] else 1
+            w = PART // cuts
             for j, c in enumerate(d["relays"]):
-                relay[c] = {"src": a, "dst": d["dst"], "table": k,
-                            "col": COLS + (CAP if d["half"] == 0 else 0) + j * PIECE}
-                d["pieces"].insert(0, {"relay": c, "off": (d["half"] * CAP + j * PIECE) // 16, "mask": topo.mask(a, c)})
+                relay[c] = {"src": a, "dst": d["dst"], "table": k, "width": w, "incs": [],
+                            "col": COLS + (CAP if d["half"] == 0 else 0) + j * PART}
                 k += 1
+            for i in range(cuts):
+                for j in (1, 0):
+                    c = d["relays"][j]
+                    d["pieces"].append({"relay": c, "off": (d["half"] * CAP + j * PART + i * w) // 16, "width": w, "cut": i,
+                                        "mask": topo.mask(a, c)})
+            came[d["dst"]] = came.get(d["dst"], 0) + 2 * cuts
         away = 0
         for d in halves:
             if not d["near"]:
                 for p in d["pieces"]:
                     away |= p["mask"]
+        one, two = halves[0]["pieces"], halves[1]["pieces"]
         if away:
-            order = [p for pair in zip(*[d["pieces"] for d in halves]) for p in pair]
+            t = len(one) // 2
+            order = one[:t] + two[:1] + one[t:] + two[1:]
             for d in halves:
                 if d["near"]:
                     for p in d["pieces"]:
                         p["mask"] &= ~away
         else:
-            order = [p for d in halves for p in d["pieces"]]
+            order = one + two
         for p in order:
-            relay[p["relay"]]["inc"] = _count(p["mask"])
+            relay[p["relay"]]["incs"].append(_count(p["mask"]))
         send[a] = order
         rest = sorted([c for c in chip if c not in used], key=lambda c: topo.die(c) != topo.die(a))
         for k in range(HELPERS):
             helper[rest[k]] = (a, k)
-    _PLAN.update({"send": send, "relay": relay, "helper": helper})
+    _PLAN.update({"send": send, "relay": relay, "helper": helper, "came": came})
     return _PLAN
 
 
@@ -269,13 +277,14 @@ def _rank(g, core, T, topo, plan):
     for q in (v, s):
         q.wait_ge(so, 1)
         q.wait_ge(sem.lx, 16)
-    for k, p in enumerate(plan["send"][core]):
+    lo = 0
+    for p in plan["send"][core]:
         done = []
+        w = p["width"]
         for j in (0, 1):
-            c = p["off"] + j * HALF
-            src = T.xs[:, 0:COLS].indirect(T.soff[:, c:c + HALF])
-            lo = k * PIECE + j * PIECE // 2
-            dst = T.stage[:, lo:lo + PIECE // 2]
+            c = p["off"] + j * w // 32
+            src = T.xs[:, 0:COLS].indirect(T.soff[:, c:c + w // 32])
+            dst = T.stage[:, lo + j * w // 2:lo + (j + 1) * w // 2]
             e = new()
             if j == 0:
                 v.tensor_copy(dst, src).then_inc(e, 1)
@@ -284,8 +293,10 @@ def _rank(g, core, T, topo, plan):
             done.append(e)
         for e in done:
             g.wait_ge(e, 1)
-        _put(g, T, topo, core, p["relay"], T.hop[:, :], T.stage[:, k * PIECE:(k + 1) * PIECE], sem.din, p["mask"])
+        at = p["cut"] * w
+        _put(g, T, topo, core, p["relay"], T.hop[:, at:at + w], T.stage[:, lo:lo + w], sem["din%d" % p["cut"]], p["mask"])
         sent += _count(p["mask"])
+        lo += w
     g.sem_inc(sem.sentb, 1)
 
     sc = _invert_scatter(g, T, new, (sem.ltile, 16), [(sem.tval, 8), (zero, 1)])
@@ -302,7 +313,7 @@ def _rank(g, core, T, topo, plan):
     for q in (v, s):
         q.wait_ge(wb, 1)
         q.wait_ge(sem.lgh, 32)
-        q.wait_ge(sem.arr, 32)
+        q.wait_ge(sem.arr, 8 * plan["came"][core])
     col = 0
     came = [set(), set()]
     for w in CHUNKS:
@@ -356,9 +367,12 @@ def _relay(g, core, T, topo, job):
         e = _make_def(g, T, new, c0, T.defs[:, :])
         g.wait_ge(e, 1)
         _put(g, T, topo, core, job["src"], T.plcdef[:, c0:c0 + TABC], T.defs[:, :], sem.tdef, m)
-    g.wait_ge(sem.din, job["inc"])
-    _put(g, T, topo, core, job["dst"], T.gat[:, job["col"]:job["col"] + PIECE], T.hop[:, :], sem.arr, m)
-    g.wait_ge(sem.loc, 2 * _count(m))
+    w = job["width"]
+    for i, n in enumerate(job["incs"]):
+        g.wait_ge(sem["din%d" % i], n)
+        _put(g, T, topo, core, job["dst"], T.gat[:, job["col"] + i * w:job["col"] + (i + 1) * w], T.hop[:, i * w:(i + 1) * w],
+             sem.arr, m)
+    g.wait_ge(sem.loc, (1 + len(job["incs"])) * _count(m))
 
 
 def _helper(g, core, T, topo, plan):

from concourse.bass import DstId, RemoteDMATransfer
from concourse.mybir import AluOpType, ActivationFunctionType

COLS = 4096
CAP = 1024
PART = 512
OWNC = 128
TABC = 64
HELPERS = 2
GH1 = 512
CHUNKS = [256, 512, 512, 512, 256]

SCRATCH = {
    "sndi": ("sbuf", [16, 128], "int32"),
    "sndf": ("sbuf", [16, 128], "float32"),
    "repi": ("sbuf", [16, 128], "int32"),
    "repa": ("sbuf", [16, 128], "int32"),
    "rep": ("sbuf", [16, 128], "float32"),
    "soff": ("sbuf", [128, 128], "uint16"),
    "xs": ("sbuf", [128, 4096], "bfloat16"),
    "stage": ("sbuf", [128, 2048], "bfloat16"),
    "gat": ("sbuf", [128, 6144], "bfloat16"),
    "ys": ("sbuf", [128, 4096], "bfloat16"),
    "wm": ("sbuf", [128, 128], "uint16"),
    "wh": ("sbuf", [128, 128], "uint16"),
    "plcd": ("dram", [128, 16], "int32"),
    "plci": ("sbuf", [128, 16], "int32"),
    "poff": ("sbuf", [128, 16], "uint16"),
    "win": ("sbuf", [128, 4096], "bfloat16"),
    "hi": ("sbuf", [128, 256], "float32"),
    "lo": ("sbuf", [128, 256], "float32"),
    "him": ("sbuf", [128, 256], "float32"),
    "lom": ("sbuf", [128, 256], "float32"),
    "val": ("sbuf", [128, 256], "bfloat16"),
    "pidx": ("sbuf", [128, 8], "int32"),
    "pmod": ("sbuf", [128, 8], "int32"),
    "pmf": ("sbuf", [128, 8], "float32"),
    "is0": ("sbuf", [128, 8], "float32"),
    "is1": ("sbuf", [128, 8], "float32"),
    "wf": ("sbuf", [128, 128], "float32"),
    "wl": ("sbuf", [128, 64], "uint16"),
    "comb": ("sbuf", [128, 144], "bfloat16"),
    "plcdef": ("sbuf", [128, 128], "float32"),
    "vals": ("sbuf", [128, 256], "bfloat16"),
    "combi": ("sbuf", [128, 144], "int32"),
    "comba": ("sbuf", [128, 144], "int32"),
    "combs": ("sbuf", [128, 144], "bfloat16"),
    "defi": ("sbuf", [128, 64], "float32"),
    "defs": ("sbuf", [128, 64], "float32"),
    "hop": ("sbuf", [128, 512], "bfloat16"),
    "psa": ("psum", [128, 512], "float32"),
    "psw": ("psum", [128, 512], "float32"),
}
SEMAPHORES = (["lsnd", "lplc", "ltile", "lx", "lgh", "st", "loc", "arr", "din0", "din1", "pin", "win0", "win1",
               "tcomb", "tval", "tdef", "sentb"] + ["c%d" % k for k in range(60)])

_PLAN = {}


def _bits(mask):
    return [1 << i for i in range(16) if (mask >> i) & 1]


def _count(mask):
    return len(_bits(mask))


def _plan(T, topo):
    if _PLAN:
        return _PLAN
    cores = [int(c) for c in T.cores]
    n = len(cores)
    world = range(512)
    send, relay, helper, came = {}, {}, {}, {}
    for r, a in enumerate(cores):
        chip = [c for c in world if c != a and topo.host(c) == topo.host(a) and topo.chip(c) == topo.chip(a)]
        halves = []
        used = set()
        for h in (0, 1):
            b = cores[(r - 1) % n] if h == 0 else cores[(r + 1) % n]
            cand = [c for c in chip if topo.may_write(c, b) and c not in used]
            if not cand:
                cand = [c for c in world if topo.same_plane(a, c) and topo.host(c) != topo.host(a)
                        and topo.may_write(a, c) and topo.may_write(c, b)
                        and any(topo.mates(c, m) and topo.chip(m) == topo.chip(b) for m in world)]
            near = [c for c in cand if topo.die(c) == topo.die(a)][0]
            far = [c for c in cand if topo.die(c) != topo.die(a)][0]
            used.update((near, far))
            halves.append({"half": h, "dst": b, "relays": [near, far],
                           "first": topo.rack(topo.host(a)) != topo.rack(topo.host(b)), "near": near in chip})
        halves.sort(key=lambda d: not d["first"])
        k = 0
        for d in sorted(halves, key=lambda d: not d["near"]):
            d["pieces"] = []
            cuts = 2 if d["first"] else 1
            w = PART // cuts
            for j, c in enumerate(d["relays"]):
                relay[c] = {"src": a, "dst": d["dst"], "table": k, "width": w, "incs": [],
                            "col": COLS + (CAP if d["half"] == 0 else 0) + j * PART}
                k += 1
            for i in range(cuts):
                for j in (1, 0):
                    c = d["relays"][j]
                    d["pieces"].append({"relay": c, "off": (d["half"] * CAP + j * PART + i * w) // 16, "width": w, "cut": i,
                                        "mask": topo.mask(a, c)})
            came[d["dst"]] = came.get(d["dst"], 0) + 2 * cuts
        away = 0
        for d in halves:
            if not d["near"]:
                for p in d["pieces"]:
                    away |= p["mask"]
        one, two = halves[0]["pieces"], halves[1]["pieces"]
        if away:
            t = len(one) // 2
            order = one[:t] + two[:1] + one[t:] + two[1:]
            for d in halves:
                if d["near"]:
                    for p in d["pieces"]:
                        p["mask"] &= ~away
        else:
            order = one + two
        for p in order:
            relay[p["relay"]]["incs"].append(_count(p["mask"]))
        send[a] = order
        rest = sorted([c for c in chip if c not in used], key=lambda c: topo.die(c) != topo.die(a))
        for k in range(HELPERS):
            helper[rest[k]] = (a, k)
    _PLAN.update({"send": send, "relay": relay, "helper": helper, "came": came})
    return _PLAN


def _seq(T):
    n = [0]

    def new():
        n[0] += 1
        return T.sem["c%d" % (n[0] - 1)]
    return new


def _ids(topo, dst, src):
    rid, pid = topo.addr(dst, src)
    return [DstId(rid=rid, pnc=pid)]


def _put(g, T, topo, src, dst, out, in_, sem, mask):
    rid, pid = topo.addr(dst, src)
    g.remote_dma(out, in_, sem, T.sem.loc, pid, rid, mask)


def _make_comb(g, T, new, out):
    v = g.vector
    a, b, c = new(), new(), new()
    g.iota(T.combi[:, :], [[1, 144]], 0, 0).then_inc(a, 1)
    v.wait_ge(a, 1)
    v.tensor_scalar(T.comba[:, :], T.combi[:, :], 15, None, AluOpType.bitwise_and).then_inc(b, 1)
    v.wait_ge(b, 1)
    v.tensor_scalar(out, T.comba[:, :], 0, None, AluOpType.is_equal).then_inc(c, 1)
    return c


def _part_mod(g, T, new):
    a, b = new(), new()
    g.iota(T.pidx[:, :], [[0, 8]], 0, 1).then_inc(a, 1)
    g.vector.wait_ge(a, 1)
    g.vector.tensor_scalar(T.pmod[:, :], T.pidx[:, :], 15, None, AluOpType.bitwise_and).then_inc(b, 1)
    g.vector.wait_ge(b, 1)


def _make_def(g, T, new, c0, out):
    v = g.vector
    a, b, c = new(), new(), new()
    g.iota(T.defi[:, :], [[16, TABC]], 16 * c0, 0, allow_small_or_imprecise_dtypes=True).then_inc(a, 1)
    v.tensor_copy(T.pmf[:, :], T.pmod[:, :]).then_inc(b, 1)
    v.wait_ge(a, 1)
    v.wait_ge(b, 1)
    v.tensor_scalar(out, T.defi[:, :], T.pmf[:, 0:1], None, AluOpType.add).then_inc(c, 1)
    return c


def _make_val_iotas(g, T, new):
    a, b = new(), new()
    g.iota(T.hi[:, :], [[0, 16], [0, 2], [256, 8]], COLS, 0, allow_small_or_imprecise_dtypes=True).then_inc(a, 1)
    g.iota(T.lo[:, :], [[128, 16], [8, 2], [0, 8]], -1, 1, allow_small_or_imprecise_dtypes=True).then_inc(b, 1)
    return a, b


def _make_val(g, T, new, a, b, out):
    v = g.vector
    c, d, e, f, h = new(), new(), new(), new(), new()
    v.tensor_scalar(T.is0[:, :], T.pmod[:, :], 0, None, AluOpType.is_equal).then_inc(c, 1)
    v.tensor_scalar(T.is1[:, :], T.pmod[:, :], 1, 0.125, AluOpType.is_equal, AluOpType.mult).then_inc(d, 1)
    v.wait_ge(a, 1)
    v.wait_ge(c, 1)
    v.tensor_scalar(T.him[:, :], T.hi[:, :], T.is0[:, 0:1], None, AluOpType.mult).then_inc(e, 1)
    v.wait_ge(b, 1)
    v.wait_ge(d, 1)
    v.tensor_scalar(T.lom[:, :], T.lo[:, :], T.is1[:, 0:1], None, AluOpType.mult).then_inc(f, 1)
    v.wait_ge(e, 1)
    v.wait_ge(f, 1)
    v.tensor_tensor(out, T.him[:, :], T.lom[:, :], AluOpType.add).then_inc(h, 1)
    return h


def _invert_scatter(g, T, new, plc, ready):
    v = g.vector
    a, b = new(), new()
    v.wait_ge(plc[0], plc[1])
    v.tensor_copy(T.poff[:, :], T.plci[:, :]).then_inc(a, 1)
    v.wait_ge(a, 1)
    for s, n in ready:
        v.wait_ge(s, n)
    v.tensor_copy(T.win[:, 0:COLS].indirect(T.poff[:, 0:16]), T.val[:, :]).then_inc(b, 1)
    return b


def _invert_matmul(g, T, new, c0, n):
    a = new()
    for q in range(16):
        lo = 16 * c0 + q
        mm = g.tensor.matmul(T.psw[:, 0:n], T.comb[:, 16 - q:144 - q], T.win[:, lo:16 * (c0 + n):16], q == 0, q == 15)
        if q == 15:
            mm.then_inc(a, 1)
    return a


def _helpers(plan, rank):
    return sorted([h for h in plan["helper"] if plan["helper"][h][0] == rank], key=lambda h: plan["helper"][h][1])


def _plc_mask(topo, rank, helpers):
    m = topo.mask(rank, helpers[0])
    for h in helpers[1:]:
        m &= topo.mask(rank, h)
    return m


def _rank(g, core, T, topo, plan):
    new = _seq(T)
    v, s, pe, sy = g.vector, g.scalar, g.tensor, g.sync
    sem = T.sem
    helpers = _helpers(plan, core)
    sy.dma_start(T.sndi[:, :], T.snd[:, :]).then_inc(sem.lsnd, 16)
    s.dma_start(T.plcd[:, :], T.plc[:, :]).then_inc(sem.lplc, 16)
    sy.dma_start(T.xs[:, :], T.x[:, :]).then_inc(sem.lx, 16)
    sy.wait_ge(sem.lsnd, 16)
    sy.dma_start(T.plci[:, :], T.plc[:, :]).then_inc(sem.ltile, 16)
    sy.dma_start(T.gat[:, 0:GH1], T.gh[:, 0:GH1]).then_inc(sem.lgh, 16)
    sy.wait_ge(sem.sentb, 1)
    sy.dma_start(T.gat[:, GH1:COLS], T.gh[:, GH1:COLS]).then_inc(sem.lgh, 16)

    zero = new()
    v.memset(T.win[:, 0:16 * OWNC], 0.0).then_inc(zero, 1)
    ri, ra, rr = new(), new(), new()
    g.iota(T.repi[:, :], [[1, 128]], 0, -1).then_inc(ri, 1)
    v.wait_ge(ri, 1)
    v.tensor_scalar(T.repa[:, :], T.repi[:, :], 15, None, AluOpType.bitwise_and).then_inc(ra, 1)
    v.wait_ge(ra, 1)
    v.tensor_scalar(T.rep[:, :], T.repa[:, :], 0, None, AluOpType.is_equal).then_inc(rr, 1)

    sf, sm, so = new(), new(), new()
    v.wait_ge(sem.lsnd, 16)
    v.tensor_copy(T.sndf[:, :], T.sndi[:, :]).then_inc(sf, 1)
    pe.wait_ge(rr, 1)
    pe.wait_ge(sf, 1)
    pe.matmul(T.psa[:, 0:128], T.rep[:, :], T.sndf[:, :], True, True).then_inc(sm, 1)
    v.wait_ge(sm, 1)
    v.tensor_copy(T.soff[:, :], T.psa[:, 0:128]).then_inc(so, 1)

    g.wait_ge(sem.lplc, 16)
    m = _plc_mask(topo, core, helpers)
    g.remote_dma_fused([RemoteDMATransfer(dst_ids=[d for h in helpers for d in _ids(topo, h, core)], dma_engine_mask=m,
                                          remote_sem=sem.pin, srcs=[T.plcd[:, :]], dsts=[T.plci[:, :] for h in helpers])],
                       local_sem=sem.loc)
    sent = _count(m)

    for q in (v, s):
        q.wait_ge(so, 1)
        q.wait_ge(sem.lx, 16)
    lo = 0
    for p in plan["send"][core]:
        done = []
        w = p["width"]
        for j in (0, 1):
            c = p["off"] + j * w // 32
            src = T.xs[:, 0:COLS].indirect(T.soff[:, c:c + w // 32])
            dst = T.stage[:, lo + j * w // 2:lo + (j + 1) * w // 2]
            e = new()
            if j == 0:
                v.tensor_copy(dst, src).then_inc(e, 1)
            else:
                s.activation(dst, src, ActivationFunctionType.Copy, bias=-0.0).then_inc(e, 1)
            done.append(e)
        for e in done:
            g.wait_ge(e, 1)
        at = p["cut"] * w
        _put(g, T, topo, core, p["relay"], T.hop[:, at:at + w], T.stage[:, lo:lo + w], sem["din%d" % p["cut"]], p["mask"])
        sent += _count(p["mask"])
        lo += w
    g.sem_inc(sem.sentb, 1)

    sc = _invert_scatter(g, T, new, (sem.ltile, 16), [(sem.tval, 8), (zero, 1)])
    pe.wait_ge(sc, 1)
    pe.wait_ge(sem.tcomb, 8)
    pw = _invert_matmul(g, T, new, 0, OWNC)
    wa, wb = new(), new()
    v.wait_ge(pw, 1)
    v.wait_ge(sem.tdef, 16)
    v.tensor_tensor(T.wf[:, :], T.psw[:, 0:OWNC], T.plcdef[:, :], AluOpType.max).then_inc(wa, 1)
    v.wait_ge(wa, 1)
    v.tensor_copy(T.wm[:, :], T.wf[:, :]).then_inc(wb, 1)

    for q in (v, s):
        q.wait_ge(wb, 1)
        q.wait_ge(sem.lgh, 32)
        q.wait_ge(sem.arr, 8 * plan["came"][core])
    col = 0
    came = [set(), set()]
    for w in CHUNKS:
        done = []
        for j in (0, 1):
            a = col + j * w
            c = a // 16
            if c < OWNC:
                off = T.wm[:, c:c + w // 16]
            else:
                c -= OWNC
                off = T.wh[:, c:c + w // 16]
                k = c // TABC
                if k not in came[j]:
                    (v, s)[j].wait_ge(sem["win%d" % k], 8)
                    came[j].add(k)
            src = T.gat[:, :].indirect(off)
            dst = T.ys[:, a:a + w]
            e = new()
            if j == 0:
                v.tensor_copy(dst, src).then_inc(e, 1)
            else:
                s.activation(dst, src, ActivationFunctionType.Copy, bias=-0.0).then_inc(e, 1)
            done.append(e)
        for e in done:
            sy.wait_ge(e, 1)
        sy.dma_start(T.y[:, col:col + 2 * w], T.ys[:, col:col + 2 * w]).then_inc(sem.st, 16)
        col += 2 * w
    sy.wait_ge(sem.st, 16 * len(CHUNKS))
    g.wait_ge(sem.loc, sent)


def _relay(g, core, T, topo, job):
    new = _seq(T)
    sem = T.sem
    m = topo.mask(core, job["dst"])
    k = job["table"]
    if k == 0:
        a, b = _make_val_iotas(g, T, new)
        _part_mod(g, T, new)
        e = _make_val(g, T, new, a, b, T.vals[:, :])
        g.wait_ge(e, 1)
        _put(g, T, topo, core, job["src"], T.val[:, :], T.vals[:, :], sem.tval, m)
    elif k == 1:
        e = _make_comb(g, T, new, T.combs[:, :])
        g.wait_ge(e, 1)
        _put(g, T, topo, core, job["src"], T.comb[:, :], T.combs[:, :], sem.tcomb, m)
    else:
        c0 = (k - 2) * TABC
        _part_mod(g, T, new)
        e = _make_def(g, T, new, c0, T.defs[:, :])
        g.wait_ge(e, 1)
        _put(g, T, topo, core, job["src"], T.plcdef[:, c0:c0 + TABC], T.defs[:, :], sem.tdef, m)
    w = job["width"]
    for i, n in enumerate(job["incs"]):
        g.wait_ge(sem["din%d" % i], n)
        _put(g, T, topo, core, job["dst"], T.gat[:, job["col"] + i * w:job["col"] + (i + 1) * w], T.hop[:, i * w:(i + 1) * w],
             sem.arr, m)
    g.wait_ge(sem.loc, (1 + len(job["incs"])) * _count(m))


def _helper(g, core, T, topo, plan):
    new = _seq(T)
    v = g.vector
    sem = T.sem
    rank, k = plan["helper"][core]
    c0 = OWNC + k * TABC
    zero = new()
    v.memset(T.win[:, 16 * c0:16 * (c0 + TABC)], 0.0).then_inc(zero, 1)
    a, b = _make_val_iotas(g, T, new)
    _part_mod(g, T, new)
    val = _make_val(g, T, new, a, b, T.val[:, :])
    comb = _make_comb(g, T, new, T.comb[:, :])
    dfl = _make_def(g, T, new, c0, T.defs[:, :])
    n = _count(_plc_mask(topo, rank, _helpers(plan, rank)))
    sc = _invert_scatter(g, T, new, (sem.pin, n), [(val, 1), (zero, 1)])
    g.tensor.wait_ge(comb, 1)
    g.tensor.wait_ge(sc, 1)
    pw = _invert_matmul(g, T, new, c0, TABC)
    wa, wb = new(), new()
    v.wait_ge(pw, 1)
    v.wait_ge(dfl, 1)
    v.tensor_tensor(T.wf[:, 0:TABC], T.psw[:, 0:TABC], T.defs[:, :], AluOpType.max).then_inc(wa, 1)
    v.wait_ge(wa, 1)
    v.tensor_copy(T.wl[:, :], T.wf[:, 0:TABC]).then_inc(wb, 1)
    g.wait_ge(wb, 1)
    m = 0
    for bit in _bits(topo.mask(core, rank))[::2]:
        m |= bit
    _put(g, T, topo, core, rank, T.wh[:, k * TABC:(k + 1) * TABC], T.wl[:, :], sem["win%d" % k], m)
    g.wait_ge(sem.loc, _count(m))


def rank_program(g, core, T, topo):
    plan = _plan(T, topo)
    if core in plan["send"]:
        _rank(g, core, T, topo, plan)
    elif core in plan["relay"]:
        _relay(g, core, T, topo, plan["relay"][core])
    elif core in plan["helper"]:
        _helper(g, core, T, topo, plan)
